import numpy as np, ml_dtypes
CORES = [36,38,116,118,124,126,164,166,244,246,252,254]
N = 12
DEG, TK, TIMES = 3, 128, 2
MASK = [[11,0,1],[0,1,2],[1,2,3],[2,3,4],[3,4,5],[4,5,6],[5,6,7],[6,7,8],[7,8,9],[8,9,10],[9,10,11],[10,11,0]]
def setup_inputs(rng):
    return {"x": rng.standard_normal((N, 128, TK), dtype=np.float32).astype(ml_dtypes.bfloat16), "w": (rng.standard_normal((N, 128, DEG * 128), dtype=np.float32) / np.float32(np.sqrt(128 * DEG / 2))).astype(ml_dtypes.bfloat16)}
def setup_inputs_big(rng):
    d = setup_inputs(rng)
    for k in ("x",): d[k] = (d[k].astype(np.float32) * 1048576.0).astype(d[k].dtype)
    return d
def setup_inputs_small(rng):
    d = setup_inputs(rng)
    for k in ("x",): d[k] = (d[k].astype(np.float32) * (1 / 1048576.0)).astype(d[k].dtype)
    return d
def setup_inputs_apart(rng):
    d = setup_inputs(rng)
    f = (10.0 ** rng.permutation(np.linspace(-1.5, 1.5, N))).astype(np.float32).reshape(N, 1, 1)
    for k in ("x",): d[k] = (d[k].astype(np.float32) * f).astype(d[k].dtype)
    return d
def reference(x, w):
    X, W = x.astype(np.float64), w.astype(np.float64)
    h = list(X)
    for _ in range(TIMES):
        h = [sum(W[r][:, 128 * i:128 * i + 128].T @ h[j] for i, j in enumerate(MASK[r])) for r in range(N)]
    return {"y": np.stack(h).astype(ml_dtypes.bfloat16)}

from concourse.bass import DstId, RemoteDMATransfer

TK = 128
NIN = 6
NOUT = 4
SCRATCH = {
    "wx": ("sbuf", [128, 4 * TK], "bfloat16"),
    "wp": ("sbuf", [128, 3 * TK], "bfloat16"),
    "inb": ("sbuf", [128, NIN * TK], "bfloat16"),
    "outb": ("sbuf", [128, NOUT * TK], "bfloat16"),
    "ps0": ("psum", [128, 512], "float32"),
    "ps1": ("psum", [128, 512], "float32"),
    "ps2": ("psum", [128, 512], "float32"),
    "ps3": ("psum", [128, 512], "float32"),
}
SEMAPHORES = (["lx", "lw", "aw", "sent", "st"] + ["a%d" % k for k in range(NIN)]
              + ["m%d" % k for k in range(NOUT)] + ["v%d" % k for k in range(NOUT)])


def _bits(mask):
    return [e for e in range(mask.bit_length()) if (mask >> e) & 1]


def _split(pool, k):
    if not k:
        return []
    share = 1
    while share * 2 * k <= len(pool):
        share *= 2
    sizes = [share] * k
    free = len(pool) - share * k
    for t in range(k):
        if free >= sizes[t]:
            free -= sizes[t]
            sizes[t] *= 2
    out, at = [], 0
    for s in sizes:
        out.append(sum(1 << e for e in pool[at:at + s]))
        at += s
    return out


def _tiles(item):
    return 3 if item[0] == "W" else 1


def _plan(T, topo):
    cores, M = list(T.cores), T.tables["MASK"]
    n = len(cores)

    def ok(a, b):
        return topo.may_write(cores[a], cores[b])

    def near(a, b):
        return (topo.host(cores[a]), topo.chip(cores[a])) == (topo.host(cores[b]), topo.chip(cores[b]))

    users = [[c for c in range(n) if j in M[c]] for j in range(n)]
    late, proxy = {}, {}
    for d in range(n):
        for i, s in enumerate(M[d]):
            if s != d and not ok(s, d):
                late[d] = (i, s)
                proxy[s] = [q for q in range(n) if q != s and near(q, s)
                            and all(ok(q, c) for c in users[d] + users[s] if c != q)][0]
    site = [proxy.get(k, k) for k in range(n)]

    stages = [[[], [], [], []] for _ in range(n)]
    for j in range(n):
        for c in sorted({site[k] for k in users[j] if late.get(k, (0, -1))[1] != j} - {j}):
            stages[j][0].append((("x", j), c))
    for s in sorted(proxy):
        stages[s][1].append((("W", s), proxy[s]))
    for d in sorted(late):
        s = late[d][1]
        for c in users[d]:
            if c != d:
                stages[d][1].append((("L", d), c))
            if c != s and c != proxy[s]:
                stages[proxy[s]][2].append((("x", s), c))
    for k in range(n):
        for c in users[k]:
            if c != site[k]:
                stages[site[k]][3].append(((("R" if k in late else "h"), k), c))

    slot, count, sender, used = {}, {}, {}, [0] * n
    calls = [[] for _ in range(n)]
    for r in range(n):
        away = [topo.mask(cores[r], cores[q]) for q in range(n) if not near(r, q) and ok(r, q)]
        home = [topo.mask(cores[r], cores[q]) for q in range(n) if q != r and near(r, q)]
        far = _bits(min(away))
        every = _bits(max(home))
        rest = [e for e in every if e not in far]
        for st in stages[r]:
            for width in (1, 3):
                tr = [t for t in st if _tiles(t[0]) == width]
                off = [t for t in tr if not near(r, t[1])]
                on = [t for t in tr if near(r, t[1])]
                pool = every if (width > 1 and not off) else rest
                todo = list(zip(off, _split(far, len(off)))) + list(zip(on, _split(pool, len(on))))
                if todo:
                    calls[r].append(todo)
                for (item, c), mask in todo:
                    count[(c, item)] = len(_bits(mask))
                    sender[(c, item)] = r
                    if width == 1:
                        slot[(c, item)] = used[c]
                        used[c] += 1
    return dict(M=M, n=n, cores=cores, near=near, late=late, proxy=proxy, site=site, calls=calls,
                slot=slot, count=count, sender=sender)


def rank_program(g, core, T, topo):
    r = T.rank_of(core)
    if r is None:
        return
    P = _plan(T, topo)
    M, late, site, near = P["M"], P["late"], P["site"], P["near"]

    made = [(("R" if k in late else "h"), k) for k in sorted(range(P["n"]), key=lambda k: k != r) if site[k] == r]
    made += [("T", d) for d in M[r] if d in late]
    made += [("y", r)]
    bank = {item: b for b, item in enumerate(made)}

    def where(item):
        kind, k = item
        if item in bank:
            b = bank[item]
            return T.outb[:, b * TK:(b + 1) * TK], "v%d" % b, 1, 0
        if k == r and kind == "x":
            return T.wx[:, 3 * TK:4 * TK], "lx", 16, 0
        if k == r and kind == "W":
            return T.wx[:, 0:3 * TK], "lw", 16, 0
        if k == r and kind == "L":
            i = late[r][0]
            return T.wx[:, i * TK:(i + 1) * TK], "lw", 16, 0
        dist = 1 if near(r, P["sender"][(r, item)]) else 2
        if kind == "W":
            return T.wp[:, 0:3 * TK], "aw", P["count"][(r, item)], dist
        a = P["slot"][(r, item)]
        return T.inb[:, a * TK:(a + 1) * TK], "a%d" % a, P["count"][(r, item)], dist

    def tile(k, i):
        if k == r:
            return T.wx[:, i * TK:(i + 1) * TK], "lw", 16, 0
        _, sem, cnt, dist = where(("W", k))
        return T.wp[:, i * TK:(i + 1) * TK], sem, cnt, dist

    def waiter(queue):
        seen = set()

        def wait(sem, cnt):
            if (sem, cnt) not in seen:
                seen.add((sem, cnt))
                queue.wait_ge(T.sem[sem], cnt)
        return wait

    g.sync.dma_start(T.wx[:, 3 * TK:4 * TK], T.x[:, :]).then_inc(T.sem.lx, 16)
    g.scalar.dma_start(T.wx[:, 0:3 * TK], T.w[:, :]).then_inc(T.sem.lw, 16)

    gwait = waiter(g)
    total = 0
    for todo in P["calls"][r]:
        trs = []
        for (item, c), mask in todo:
            src, sem, cnt, _ = where(item)
            gwait(sem, cnt)
            rid, pid = topo.addr(P["cores"][c], core)
            if item[0] == "W":
                dst, rsem = T.wp[:, 0:3 * TK], "aw"
            else:
                a = P["slot"][(c, item)]
                dst, rsem = T.inb[:, a * TK:(a + 1) * TK], "a%d" % a
            trs.append(RemoteDMATransfer(dst_ids=[DstId(rid=rid, pnc=pid)], dma_engine_mask=mask,
                                         remote_sem=T.sem[rsem], src=src, dst=dst))
            total += len(_bits(mask))
        g.remote_dma_fused(trs, local_sem=T.sem.sent)

    seq = []
    for item in made:
        if item[0] in ("h", "R"):
            k = item[1]
            terms = [(i, j) for i, j in enumerate(M[k]) if not (k in late and late[k][0] == i)]
            for i, j in sorted(terms, key=lambda t: where(("x", t[1]))[3]):
                seq.append((item, tile(k, i), where(("x", j))))
    mine = [d for d in M[r] if d in late and late[d][1] == r]
    fwd = [d for d in M[r] if d in late and late[d][1] != r]
    for d in mine:
        seq.append((("T", d), where(("L", d)), where(("x", r))))
    y = ("y", r)
    parts = []
    for i, j in enumerate(M[r]):
        parts += [(i, ("R", j)), (i, ("T", j))] if j in late else [(i, ("h", j))]
    early = [p for p in parts if where(p[1])[3] == 0 and not (p[1][0] == "T" and p[1][1] in fwd)]
    for i, item in early:
        seq.append((y, tile(r, i), where(item)))
    for d in fwd:
        seq.append((("T", d), where(("L", d)), where(("x", late[d][1]))))
    for i, item in parts:
        if item[0] == "T" and item[1] in fwd:
            seq.append((y, tile(r, i), where(item)))
    for i, item in sorted([p for p in parts if where(p[1])[3] > 0], key=lambda p: where(p[1])[3]):
        seq.append((y, tile(r, i), where(item)))

    first = {}
    last = {}
    for at, (grp, _, _) in enumerate(seq):
        first.setdefault(grp, at)
        last[grp] = at
    twait = waiter(g.tensor)
    for at, (grp, lhs, rhs) in enumerate(seq):
        twait(lhs[1], lhs[2])
        twait(rhs[1], rhs[2])
        b = bank[grp]
        mm = g.tensor.matmul(T["ps%d" % b][:, 0:TK], lhs[0], rhs[0], first[grp] == at, last[grp] == at)
        if last[grp] == at:
            mm.then_inc(T.sem["m%d" % b], 1)

    for grp in sorted(last, key=lambda q: last[q]):
        b = bank[grp]
        g.vector.wait_ge(T.sem["m%d" % b], 1)
        g.vector.tensor_copy(T.outb[:, b * TK:(b + 1) * TK], T["ps%d" % b][:, 0:TK]).then_inc(T.sem["v%d" % b], 1)

    b = bank[y]
    g.sync.wait_ge(T.sem["v%d" % b], 1)
    g.sync.dma_start(T.y[:, :], T.outb[:, b * TK:(b + 1) * TK]).then_inc(T.sem.st, 16)
    g.sync.wait_ge(T.sem.st, 16)
    if total:
        g.wait_ge(T.sem.sent, total)
